import numpy as np
import ml_dtypes


def mxq(x, axis, fmt="e4m3"):
    dtype, down = {"e4m3": (ml_dtypes.float8_e4m3fn, 7), "e5m2": (ml_dtypes.float8_e5m2, 14)}[fmt]
    v = np.moveaxis(np.asarray(x, np.float32).astype(ml_dtypes.bfloat16).astype(np.float64), axis, -1)
    blocks = v.reshape(v.shape[:-1] + (-1, 32))
    amax = np.abs(blocks).max(-1, keepdims=True)
    byte = np.maximum(np.where(amax > 0, np.frexp(amax)[1] - 1 + 127, 0) - down, 1)
    scale = np.exp2(byte - 127.0)
    codes = (blocks / scale).astype(np.float32).astype(dtype).astype(np.float64)
    return np.moveaxis((codes * scale).reshape(v.shape), -1, axis)


WIDE = False


def mx_kscale(k):
    if not WIDE:
        return np.ones(k)
    levels = np.array([10, -10, 5, -5, 0])
    if k % 512:
        return np.exp2(np.random.permutation(np.resize(levels, k // 32))).repeat(32)
    a = np.empty((k // 512, 16))
    for p in range(k // 512):
        a[p, :8] = np.random.permutation(np.resize(levels, 8))
        for g in range(8):
            far = levels[np.abs(levels - a[p, g]) >= 10]
            a[p, g + 8] = far[np.random.randint(len(far))]
    return np.exp2(a.ravel()).repeat(32)


def f64(x):
    return np.asarray(x).astype(np.float64)


def striped(idx):
    return np.tile(idx.reshape(-1, 16).T, (8, 1)).astype(np.uint16)


def unstriped(offs):
    return offs[:16].T.reshape(-1).astype(np.int64)


E2M1 = np.array([0.0, 0.5, 1.0, 1.5, 2.0, 3.0, 4.0, 6.0, -0.0, -0.5, -1.0, -1.5, -2.0, -3.0, -4.0, -6.0])


def pack_weight(w, fmt):
    k, n = w.shape
    w = f64(np.asarray(w, np.float32).astype(ml_dtypes.bfloat16)).reshape(k // 32, 32, n)
    amax = np.abs(w).max(1)
    if fmt == "e4m3":
        byte = np.frexp(amax)[1] - 1 + 127 - 7
    else:
        mant, ex = np.frexp(amax / 6.0)
        byte = np.where(mant > 0.5, ex, ex - 1) + 127
    byte = np.clip(np.where(amax > 0, byte, 1), 1, 254)
    scaled = (w * np.exp2(127.0 - byte)[:, None, :]).reshape(k, n).astype(np.float32)
    by_word = np.ascontiguousarray(scaled.reshape(k // 512, 128, 4, n).transpose(0, 1, 3, 2))
    if fmt == "e4m3":
        words = by_word.astype(ml_dtypes.float8_e4m3fn).view(np.uint8)
    else:
        c = by_word.astype(ml_dtypes.float4_e2m1fn).view(np.uint8) & 0xF
        words = (c[..., 0::2] | (c[..., 1::2] << 4)).reshape(k // 512, 128, 2 * n)
    return np.ascontiguousarray(words), np.ascontiguousarray(byte.astype(np.uint8).reshape(k // 512, 16, n))


def unpack_weight(words, scales, fmt):
    g, _, n = scales.shape
    words = np.ascontiguousarray(words).reshape(g, 128, n, -1)
    if fmt == "e4m3":
        vals = words.view(ml_dtypes.float8_e4m3fn).astype(np.float64)
    else:
        nib = np.empty((g, 128, n, 4), np.uint8)
        nib[..., 0::2] = words & 0xF
        nib[..., 1::2] = words >> 4
        vals = E2M1[nib]
    vals = vals * np.repeat(np.exp2(scales.astype(np.float64) - 127.0), 8, axis=1)[..., None]
    return vals.transpose(0, 1, 3, 2).reshape(g * 512, n)


def gelu(v):
    return 0.5 * v * (1.0 + np.tanh(np.sqrt(2.0 / np.pi) * (v + 0.044715 * v**3)))


def bf(x):
    return np.asarray(x, np.float32).astype(ml_dtypes.bfloat16)


def planes(Y):
    n, m = Y.shape
    b = f64(bf(Y)).reshape(n // 32, 32, m)
    amax = np.abs(b).max(1)
    byte = np.clip(np.where(amax > 0, np.frexp(amax)[1] - 1 + 127 - 7, 1), 1, 254)
    codes = (b * np.exp2(127.0 - byte)[:, None, :]).reshape(n, m).astype(np.float32).astype(ml_dtypes.float8_e4m3fn).view(np.uint8)
    words = codes.reshape(n // 512, 128, 4, m).transpose(0, 1, 3, 2)
    return np.ascontiguousarray(words), np.ascontiguousarray(byte.astype(np.uint8).reshape(n // 512, 16, m))


K, H, T, S, P, P2 = 1024, 1024, 4096, 2048, 1024, 512

def setup_inputs():
    n = np.random.standard_normal
    s = mx_kscale(K)[:, None]
    u = mx_kscale(H)[:, None]
    size = np.exp(0.8 * n(H))
    tab_words, tab_scales = pack_weight(n((K, T)) * s, "e4m3")
    w4_words, w4_scales = pack_weight(n((H, H)) / np.sqrt(H) / u * size[None, :], "e2m1")
    return {
        "tab_words": tab_words, "tab_scales": tab_scales,
        "offs": striped(np.random.permutation(T)[:S]),
        "pos1": striped(np.random.permutation(S)[:P]),
        "pos2": striped(np.random.permutation(S)[:P]),
        "pos3": striped(np.random.permutation(P)[:P2]),
        "pos4": striped(np.random.permutation(S)[:P2]),
        "w1": (1.4 * n((K, H)) / np.sqrt(K) / s).astype(np.float32),
        "gain": (1.2 * np.exp(0.3 * n(H)) * u[:, 0]).astype(np.float32),
        "link": n((H, P)).astype(np.float32),
        "w4_words": w4_words, "w4_scales": w4_scales,
        "skip": (np.exp(0.3 * n(H)) * size / u[:, 0]).astype(np.float32),
    }

def reference(tab_words, tab_scales, offs, pos1, pos2, pos3, pos4, w1, gain, link, w4_words, w4_scales, skip):
    v = unpack_weight(tab_words, tab_scales, "e4m3")[:, unstriped(offs)]
    w4 = unpack_weight(w4_words, w4_scales, "e2m1")
    x = mxq(f64(w1), 0, "e4m3").T @ v
    gelu = 0.5 * x * (1.0 + np.tanh(np.sqrt(2.0 / np.pi) * (x + 0.044715 * x ** 3)))
    h = f64(gain)[:, None] * gelu
    a1 = (h[:, unstriped(pos1)] - h[:, unstriped(pos2)]) * f64(link)
    a2 = np.maximum(a1[:, unstriped(pos3)], h[:, unstriped(pos4)])
    y = (w4.T @ mxq(a2, 0, "e4m3")) + f64(skip)[:, None] * a2
    words, scales = planes(y)
    return y, words, scales

@@ -1,0 +1,295 @@
+from contextlib import ExitStack
+
+import concourse.mybir as mybir
+
+K, H, T, S, PAIRS, KEPT = 1024, 1024, 4096, 2048, 1024, 512
+FLOPS = 2 * K * H * S + 2 * H * H * KEPT
+
+F32 = mybir.dt.float32
+BF16 = mybir.dt.bfloat16
+I32 = mybir.dt.int32
+U32 = mybir.dt.uint32
+U16 = mybir.dt.uint16
+U8 = mybir.dt.uint8
+FP8X4 = mybir.dt.float8_e4m3fn_x4
+FP4X4 = mybir.dt.float4_e2m1fn_x4
+ALU = mybir.AluOpType
+ACT = mybir.ActivationFunctionType
+
+P = 128
+PACK = 4
+PASS = P * PACK
+PASSES = 2
+BANK = 512
+CHUNKS = S // BANK
+TILES = H // P
+HELD = 4
+
+
+def tile_list_provenance_chain_features_kernel(
+    tc, tab_words, tab_scales, offs, pos1, pos2, pos3, pos4, w1, gain, link, w4_words, w4_scales, skip,
+    out_0, out_1, out_2,
+):
+    nc = tc.nc
+    with ExitStack() as ctx:
+        keep = ctx.enter_context(tc.tile_pool(name="keep", bufs=1))
+        ring = ctx.enter_context(tc.tile_pool(name="ring", bufs=1))
+        psum = ctx.enter_context(tc.psum_pool(name="psum", bufs=1))
+
+        def load_list(name, source):
+            tile = keep.tile(list(source.shape), U16, name=name)
+            nc.sync.dma_start(tile[:], source)
+            return tile
+
+        def load_table_words(a):
+            tile = ring.tile([P, T], U32, name="tab_words%d" % a, tag="wide", bufs=2, align_bytes=64)
+            words = tab_words[a].rearrange("p t i -> p (t i)").bitcast(I32)
+            for half in range(2):
+                cols = slice(half * T // 2, (half + 1) * T // 2)
+                nc.sync.dma_start(tile[:].bitcast(I32)[:, cols], words[:, cols])
+            return tile
+
+        def load_w1(a, b, pieces=1):
+            tile = ring.tile([P, PACK, PASS], F32, name="w1_%d%d" % (a, b), tag="rows", bufs=4, align_bytes=64)
+            rows = w1[a * PASS : (a + 1) * PASS, b * PASS : (b + 1) * PASS]
+            rows = rows.rearrange("(p j) n -> p j n", j=PACK)
+            for piece in range(pieces):
+                cols = slice(piece * PASS // pieces, (piece + 1) * PASS // pieces)
+                nc.sync.dma_start(tile[:, :, cols], rows[:, :, cols])
+            return tile
+
+        def load_per_row(name, source):
+            tile = keep.tile([P, TILES], F32, name=name)
+            nc.sync.dma_start(
+                tile[:].rearrange("p (b t) -> p b t", t=PACK), source.rearrange("(b p t) -> p b t", p=P, t=PACK)
+            )
+            return tile
+
+        def load_link(b):
+            tile = ring.tile([P, PACK, PAIRS], F32, name="link%d" % b, tag="wide", bufs=2, align_bytes=64)
+            nc.sync.dma_start(tile[:], link[b * PASS : (b + 1) * PASS, :].rearrange("(p t) m -> p t m", t=PACK))
+            return tile
+
+        tab_plane = keep.tile([P, T], U8, name="tab_plane", align_bytes=64)
+        nc.vector.memset(tab_plane[:].bitcast(I32)[:, : T // 8], 0)
+        nc.gpsimd.memset(tab_plane[:].bitcast(I32)[:, T // 8 :], 0)
+        for quad in range(4):
+            nc.sync.dma_start(
+                tab_plane[32 * quad : 32 * quad + 8, :].bitcast(I32),
+                tab_scales[:, 4 * quad : 4 * quad + 4, :].bitcast(I32),
+            )
+        w4_plane_raw = keep.tile([P, PASSES, H], U8, name="w4_plane_raw", align_bytes=64)
+        nc.gpsimd.memset(w4_plane_raw[:].bitcast(I32), 0)
+
+        idx = load_list("idx", offs)
+        gain_sb = load_per_row("gain_sb", gain)
+        p2 = load_list("p2", pos2)
+        p4 = load_list("p4", pos4)
+        tab_w = [load_table_words(0)]
+        p1 = load_list("p1", pos1)
+        p3 = load_list("p3", pos3)
+        skip_sb = load_per_row("skip_sb", skip)
+        w1_raw = {(0, 0): load_w1(0, 0)}
+        tab_w.append(load_table_words(1))
+        w1_raw[(1, 0)] = load_w1(1, 0, pieces=2)
+        for quad in range(4):
+            nc.sync.dma_start(
+                w4_plane_raw[32 * quad : 32 * quad + 4, :, :].bitcast(I32),
+                w4_scales[:, 4 * quad : 4 * quad + 4, :].rearrange("a r n -> r a n").bitcast(I32),
+            )
+
+        banks = [psum.tile([P, BANK], F32, name="bank%d" % n) for n in range(8)]
+
+        got_w0 = keep.tile([P, S], U32, name="got_w0", align_bytes=64)
+        nc.vector.tensor_copy(got_w0[:], tab_w[0][:].indirect(idx[:]))
+        got_plane = keep.tile([P, S], U8, name="got_plane", align_bytes=64)
+        nc.vector.tensor_copy(got_plane[:], tab_plane[:].indirect(idx[:]))
+
+        w1_codes, w1_plane = {}, {}
+
+        def quantize_w1(a, b, u, pieces=1, room=None):
+            if room is None:
+                room = ring.tile([P, BANK], F32, name="w1_grouped", tag="w1_grouped", bufs=3, align_bytes=64)
+            grouped = room[:].bitcast(BF16)
+            for piece in range(pieces):
+                qs = slice(piece * P // pieces, (piece + 1) * P // pieces)
+                nc.scalar.copy(
+                    grouped.rearrange("p (t q j) -> p q j t", t=2, j=PACK)[:, qs],
+                    w1_raw[(a, b)][:].rearrange("p j (q t) -> p q j t", t=PACK)[:, qs, :, 2 * u : 2 * u + 2],
+                )
+            codes = keep.tile([P, 2 * P], U32, name="w1_codes%d%d%d" % (a, b, u), align_bytes=64)
+            plane = keep.tile([P, 2 * P], U8, name="w1_plane%d%d%d" % (a, b, u), align_bytes=64)
+            nc.vector.quantize_mx(
+                out=codes[:].bitcast(FP8X4), scales=plane[:], in_=grouped
+            )
+            w1_codes[(a, b, u)] = codes
+            w1_plane[(a, b, u)] = plane
+
+        got_w1 = []
+
+        def pick_words_of_pass_1(c, tile):
+            nc.vector.tensor_copy(tile[:], tab_w[1][:].indirect(idx[:, c * (BANK // 16) : (c + 1) * (BANK // 16)]))
+            got_w1.append(tile)
+
+        quantize_w1(0, 0, 0)
+        for c in range(CHUNKS - 1):
+            pick_words_of_pass_1(c, keep.tile([P, BANK], U32, name="got_w1_%d" % c, align_bytes=64))
+        quantize_w1(1, 0, 0, pieces=2, room=keep.tile([P, BANK], F32, name="first_room", tag="handover", align_bytes=64))
+        pick_words_of_pass_1(CHUNKS - 1, keep.tile([P, BANK], U32, name="got_w1_last", tag="handover", align_bytes=64))
+
+        link_sb = [load_link(0)]
+        w1_raw[(0, 1)] = load_w1(0, 1)
+        w1_raw[(1, 1)] = load_w1(1, 1)
+        w4_raw = keep.tile([P, PASSES, 2 * H], U8, name="w4_raw", align_bytes=64)
+        nc.sync.dma_start(w4_raw[:].bitcast(I32), w4_words.rearrange("a p n -> p a n").bitcast(I32))
+        link_sb.append(load_link(1))
+
+        spare = [keep.tile([P, BANK], F32, name="spare%d" % n, align_bytes=64) for n in range(HELD)]
+        h = []
+
+        def first_stage(i):
+            b, t = divmod(i, PACK)
+            u, cols = t // 2, slice((t % 2) * P, (t % 2 + 1) * P)
+            h_i = ring.tile([P, S], F32, name="h", tag="h", bufs=HELD)
+            for c in range(CHUNKS):
+                bank = banks[(CHUNKS * i + c) % 8]
+                chunk = slice(c * BANK, (c + 1) * BANK)
+                for a in range(PASSES):
+                    words = got_w0[:, chunk] if a == 0 else got_w1[c][:]
+                    nc.tensor.matmul_mx(
+                        out=bank[:],
+                        lhsT=w1_codes[(a, b, u)][:, cols].bitcast(FP8X4),
+                        lhsT_scale=w1_plane[(a, b, u)][:, cols],
+                        rhs=words.bitcast(FP8X4),
+                        rhs_scale=got_plane[4 * a : P, chunk],
+                        start=(a == 0),
+                        stop=(a == PASSES - 1),
+                    )
+                if i == 0:
+                    curved = spare[(c + 1) % HELD]
+                elif c == CHUNKS - 1:
+                    curved = spare[i % HELD]
+                else:
+                    curved = ring.tile([P, BANK], F32, name="curved", tag="curved", bufs=2)
+                nc.scalar.activation(curved[:], bank[:], ACT.Gelu_apprx_tanh)
+                if i == 0:
+                    nc.vector.tensor_scalar(h_i[:, chunk], curved[:], gain_sb[:, 0:1], None, ALU.mult)
+                else:
+                    nc.scalar.activation(h_i[:, chunk], curved[:], ACT.Copy, scale=gain_sb[:, i : i + 1])
+            h.append(h_i)
+
+        second = keep.tile([P, PAIRS], F32, name="second")
+        diff = keep.tile([P, PAIRS], F32, name="diff")
+        a1 = keep.tile([P, PAIRS], F32, name="a1")
+        entry = keep.tile([P, KEPT], F32, name="entry")
+        a2 = [keep.tile([P, PACK, KEPT], F32, name="a2_%d" % b) for b in range(PASSES)]
+
+        def pick_second(i):
+            nc.vector.tensor_copy(second[:], h[i][:].indirect(p2[:]))
+
+        def pick_first_minus_second(i):
+            nc.vector.tensor_tensor(diff[:], h[i][:].indirect(p1[:]), second[:], ALU.subtract)
+
+        def times_link(i):
+            nc.vector.tensor_tensor(a1[:], diff[:], link_sb[i // PACK][:, i % PACK, :], ALU.mult)
+
+        def pick_entry(i):
+            nc.vector.tensor_copy(entry[:], h[i][:].indirect(p4[:]))
+
+        def pick_kept(i):
+            nc.vector.tensor_copy(spare[(i + 1) % HELD][:], a1[:].indirect(p3[:]))
+
+        def larger(i):
+            nc.vector.tensor_tensor(a2[i // PACK][:, i % PACK, :], spare[(i + 1) % HELD][:], entry[:], ALU.max)
+
+        def interleave(copy, grouped, planar, cols):
+            copy(
+                grouped[:, cols, :].rearrange("p (c e) t -> p c t e", e=4),
+                planar[:, :, cols].rearrange("p t (c e) -> p c t e", e=4),
+            )
+
+        a2_codes = [keep.tile([P, KEPT], U32, name="a2_codes%d" % b, align_bytes=64) for b in range(PASSES)]
+        a2_plane = [keep.tile([P, KEPT], U8, name="a2_plane%d" % b, align_bytes=64) for b in range(PASSES)]
+
+        def quantize(codes, plane, grouped):
+            nc.vector.quantize_mx(out=codes.bitcast(FP8X4), scales=plane, in_=grouped[:].rearrange("p m t -> p (m t)"))
+
+        def second_stage_pass(a):
+            for i in range(TILES):
+                nc.tensor.matmul_mx(
+                    out=banks[i][:],
+                    lhsT=w4_codes[:, a, 2 * P * i : 2 * P * (i + 1)].bitcast(FP4X4),
+                    lhsT_scale=w4_plane[:, a, P * i : P * (i + 1)],
+                    rhs=a2_codes[a][:].bitcast(FP8X4),
+                    rhs_scale=a2_plane[a][:],
+                    start=(a == 0),
+                    stop=(a == PASSES - 1),
+                )
+
+        first_stage(0)
+        quantize_w1(0, 0, 1)
+        quantize_w1(1, 0, 1, room=spare[2])
+        w4_plane = keep.tile([P, PASSES, H], U8, name="w4_plane", align_bytes=64)
+        nc.vector.tensor_copy(
+            w4_plane[:].rearrange("p a (b t q) -> p (a b) t q", t=PACK, q=P),
+            w4_plane_raw[:].rearrange("p a (b q t) -> p (a b) t q", t=PACK, q=P),
+        )
+        pick_second(0)
+        pick_entry(0)
+        pick_first_minus_second(0)
+        times_link(0)
+
+        everything = slice(0, KEPT)
+        for i in range(TILES - 1):
+            first_stage(i + 1)
+            if i < 2:
+                quantize_w1(0, 1, i)
+                quantize_w1(1, 1, i)
+            if i == TILES - 2:
+                w4_codes = keep.tile([P, PASSES, 2 * H], U8, name="w4_codes", align_bytes=64)
+                nc.scalar.copy(
+                    w4_codes[:].bitcast(U16).rearrange("p a (b t q) -> p (a b) t q", t=PACK, q=P),
+                    w4_raw[:].bitcast(U16).rearrange("p a (b q t) -> p (a b) t q", t=PACK, q=P),
+                )
+                grouped = ring.tile([P, KEPT, PACK], BF16, name="grouped", tag="grouped", bufs=2, align_bytes=64)
+                interleave(nc.scalar.copy, grouped, a2[0], everything)
+            pick_second(i + 1)
+            pick_kept(i)
+            pick_first_minus_second(i + 1)
+            larger(i)
+            times_link(i + 1)
+            pick_entry(i + 1)
+        quantize(a2_codes[0][:], a2_plane[0][:], grouped)
+        second_stage_pass(0)
+        pick_kept(TILES - 1)
+        larger(TILES - 1)
+
+        grouped = ring.tile([P, KEPT, PACK], BF16, name="grouped", tag="grouped", bufs=2, align_bytes=64)
+        interleave(nc.scalar.copy, grouped, a2[1], slice(0, 192))
+        interleave(nc.vector.tensor_copy, grouped, a2[1], slice(192, KEPT))
+        quantize(a2_codes[1][:], a2_plane[1][:], grouped)
+        second_stage_pass(1)
+
+        y = [ring.tile([P, PACK, KEPT], F32, name="y%d" % b, tag="rows", bufs=4, align_bytes=64) for b in range(PASSES)]
+        y_codes = [keep.tile([P, KEPT], U32, name="y_codes%d" % b, align_bytes=64) for b in range(PASSES)]
+        y_plane = keep.tile([P, PASSES, KEPT], U8, name="y_plane", align_bytes=64)
+        y_grouped = []
+        for b in range(PASSES):
+            rows = out_0[b * PASS : (b + 1) * PASS, :].rearrange("(p t) j -> p t j", t=PACK)
+            for t in range(PACK):
+                i = PACK * b + t
+                nc.vector.scalar_tensor_tensor(
+                    y[b][:, t, :], a2[b][:, t, :], skip_sb[:, i : i + 1], banks[i][:], ALU.mult, ALU.add
+                )
+                nc.sync.dma_start(rows[:, t, :], y[b][:, t, :])
+            y_grouped.append(ring.tile([P, KEPT, PACK], BF16, name="grouped", tag="grouped", bufs=2, align_bytes=64))
+            interleave(nc.scalar.copy if b == 0 else nc.vector.tensor_copy, y_grouped[b], y[b], everything)
+        for b in range(PASSES):
+            quantize(y_codes[b][:], y_plane[:, b, :], y_grouped[b])
+            nc.sync.dma_start(out_1[b].rearrange("p m t -> p (m t)").bitcast(I32), y_codes[b][:].bitcast(I32))
+        for quad in range(4):
+            queue = nc.scalar if quad % 2 else nc.sync
+            queue.dma_start(
+                out_2[:, 4 * quad : 4 * quad + 4, :].rearrange("g r m -> r g m").bitcast(I32),
+                y_plane[32 * quad : 32 * quad + 4, :, :].bitcast(I32),
+            )

@@ -78,8 +78,10 @@ def tile_list_provenance_chain_features_kernel(
                 tab_plane[32 * quad : 32 * quad + 8, :].bitcast(I32),
                 tab_scales[:, 4 * quad : 4 * quad + 4, :].bitcast(I32),
             )
-        w4_plane_raw = keep.tile([P, PASSES, H], U8, name="w4_plane_raw", align_bytes=64)
-        nc.gpsimd.memset(w4_plane_raw[:].bitcast(I32), 0)
+        w4_rows = keep.tile([P, PASS], U8, name="w4_rows", align_bytes=64)
+        nc.gpsimd.memset(w4_rows[:].bitcast(I32), 0)
+        w4_plane = keep.tile([P, PASSES, PASSES, PASS], U8, name="w4_plane", align_bytes=64)
+        nc.gpsimd.memset(w4_plane[:].bitcast(I32), 0)
 
         idx = load_list("idx", offs)
         gain_sb = load_per_row("gain_sb", gain)
@@ -94,8 +96,8 @@ def tile_list_provenance_chain_features_kernel(
         w1_raw[(1, 0)] = load_w1(1, 0, pieces=2)
         for quad in range(4):
             nc.sync.dma_start(
-                w4_plane_raw[32 * quad : 32 * quad + 4, :, :].bitcast(I32),
-                w4_scales[:, 4 * quad : 4 * quad + 4, :].rearrange("a r n -> r a n").bitcast(I32),
+                w4_rows[32 * quad : 32 * quad + 16, :].bitcast(I32),
+                w4_scales[:, 4 * quad : 4 * quad + 4, :].rearrange("a r (b n) -> (r b) a n", n=PASS).bitcast(I32),
             )
 
         banks = [psum.tile([P, BANK], F32, name="bank%d" % n) for n in range(8)]
@@ -107,7 +109,7 @@ def tile_list_provenance_chain_features_kernel(
 
         w1_codes, w1_plane = {}, {}
 
-        def quantize_w1(a, b, u, pieces=1, room=None):
+        def round_w1(a, b, u, pieces=1, room=None):
             if room is None:
                 room = ring.tile([P, BANK], F32, name="w1_grouped", tag="w1_grouped", bufs=3, align_bytes=64)
             grouped = room[:].bitcast(BF16)
@@ -117,11 +119,13 @@ def tile_list_provenance_chain_features_kernel(
                     grouped.rearrange("p (t q j) -> p q j t", t=2, j=PACK)[:, qs],
                     w1_raw[(a, b)][:].rearrange("p j (q t) -> p q j t", t=PACK)[:, qs, :, 2 * u : 2 * u + 2],
                 )
-            codes = keep.tile([P, 2 * P], U32, name="w1_codes%d%d%d" % (a, b, u), align_bytes=64)
+            return grouped
+
+        def quantize_w1(a, b, u, grouped):
+            tag = "late%d%d" % (a, u) if b == 1 else "early%d%d" % (a, u)
+            codes = keep.tile([P, 2 * P], U32, name="w1_codes", tag=tag, align_bytes=64)
             plane = keep.tile([P, 2 * P], U8, name="w1_plane%d%d%d" % (a, b, u), align_bytes=64)
-            nc.vector.quantize_mx(
-                out=codes[:].bitcast(FP8X4), scales=plane[:], in_=grouped
-            )
+            nc.vector.quantize_mx(out=codes[:].bitcast(FP8X4), scales=plane[:], in_=grouped)
             w1_codes[(a, b, u)] = codes
             w1_plane[(a, b, u)] = plane
 
@@ -131,10 +135,11 @@ def tile_list_provenance_chain_features_kernel(
             nc.vector.tensor_copy(tile[:], tab_w[1][:].indirect(idx[:, c * (BANK // 16) : (c + 1) * (BANK // 16)]))
             got_w1.append(tile)
 
-        quantize_w1(0, 0, 0)
+        quantize_w1(0, 0, 0, round_w1(0, 0, 0))
         for c in range(CHUNKS - 1):
             pick_words_of_pass_1(c, keep.tile([P, BANK], U32, name="got_w1_%d" % c, align_bytes=64))
-        quantize_w1(1, 0, 0, pieces=2, room=keep.tile([P, BANK], F32, name="first_room", tag="handover", align_bytes=64))
+        first_room = keep.tile([P, BANK], F32, name="first_room", tag="handover", align_bytes=64)
+        quantize_w1(1, 0, 0, round_w1(1, 0, 0, pieces=2, room=first_room))
         pick_words_of_pass_1(CHUNKS - 1, keep.tile([P, BANK], U32, name="got_w1_last", tag="handover", align_bytes=64))
 
         link_sb = [load_link(0)]
@@ -144,7 +149,8 @@ def tile_list_provenance_chain_features_kernel(
         nc.sync.dma_start(w4_raw[:].bitcast(I32), w4_words.rearrange("a p n -> p a n").bitcast(I32))
         link_sb.append(load_link(1))
 
-        spare = [keep.tile([P, BANK], F32, name="spare%d" % n, align_bytes=64) for n in range(HELD)]
+        spare = [keep.tile([P, BANK], F32, name="spare%d" % n, align_bytes=64) for n in range(CHUNKS)]
+        a2 = [keep.tile([P, PACK, KEPT], F32, name="a2_%d" % b) for b in range(PASSES)]
         h = []
 
         def first_stage(i):
@@ -166,23 +172,25 @@ def tile_list_provenance_chain_features_kernel(
                         stop=(a == PASSES - 1),
                     )
                 if i == 0:
-                    curved = spare[(c + 1) % HELD]
-                elif c == CHUNKS - 1:
-                    curved = spare[i % HELD]
+                    curved = spare[c][:]
+                elif i >= 2 and c == CHUNKS - 1:
+                    curved = a2[(i - 2) // PACK][:, (i - 2) % PACK, :]
+                elif i in (2, 3) and c in (1, 2):
+                    curved = keep.tile([P, BANK], F32, name="curved", tag="late%d%d" % (c - 1, i - 2), align_bytes=64)[:]
                 else:
-                    curved = ring.tile([P, BANK], F32, name="curved", tag="curved", bufs=2)
-                nc.scalar.activation(curved[:], bank[:], ACT.Gelu_apprx_tanh)
+                    curved = ring.tile([P, BANK], F32, name="curved", tag="curved", bufs=2)[:]
+                nc.scalar.activation(curved, bank[:], ACT.Gelu_apprx_tanh)
                 if i == 0:
-                    nc.vector.tensor_scalar(h_i[:, chunk], curved[:], gain_sb[:, 0:1], None, ALU.mult)
+                    nc.vector.tensor_scalar(h_i[:, chunk], curved, gain_sb[:, 0:1], None, ALU.mult)
                 else:
-                    nc.scalar.activation(h_i[:, chunk], curved[:], ACT.Copy, scale=gain_sb[:, i : i + 1])
+                    nc.scalar.activation(h_i[:, chunk], curved, ACT.Copy, scale=gain_sb[:, i : i + 1])
             h.append(h_i)
 
         second = keep.tile([P, PAIRS], F32, name="second")
-        diff = keep.tile([P, PAIRS], F32, name="diff")
-        a1 = keep.tile([P, PAIRS], F32, name="a1")
-        entry = keep.tile([P, KEPT], F32, name="entry")
-        a2 = [keep.tile([P, PACK, KEPT], F32, name="a2_%d" % b) for b in range(PASSES)]
+        diff = keep.tile([P, PAIRS], F32, name="diff", tag="diff", align_bytes=64)
+        kept = [keep.tile([P, KEPT], F32, name="kept")] * (TILES - 1) + [spare[2]]
+        entry = [keep.tile([P, KEPT], F32, name="entry")] * (TILES - 1) + [spare[0]]
+        a1 = []
 
         def pick_second(i):
             nc.vector.tensor_copy(second[:], h[i][:].indirect(p2[:]))
@@ -191,16 +199,17 @@ def tile_list_provenance_chain_features_kernel(
             nc.vector.tensor_tensor(diff[:], h[i][:].indirect(p1[:]), second[:], ALU.subtract)
 
         def times_link(i):
-            nc.vector.tensor_tensor(a1[:], diff[:], link_sb[i // PACK][:, i % PACK, :], ALU.mult)
+            a1.append(ring.tile([P, PAIRS], F32, name="a1", tag="a1", bufs=2))
+            nc.gpsimd.tensor_tensor(a1[i][:], diff[:], link_sb[i // PACK][:, i % PACK, :], ALU.mult)
 
         def pick_entry(i):
-            nc.vector.tensor_copy(entry[:], h[i][:].indirect(p4[:]))
+            nc.vector.tensor_copy(entry[i][:], h[i][:].indirect(p4[:]))
 
         def pick_kept(i):
-            nc.vector.tensor_copy(spare[(i + 1) % HELD][:], a1[:].indirect(p3[:]))
+            nc.vector.tensor_copy(kept[i][:], a1[i][:].indirect(p3[:]))
 
         def larger(i):
-            nc.vector.tensor_tensor(a2[i // PACK][:, i % PACK, :], spare[(i + 1) % HELD][:], entry[:], ALU.max)
+            nc.vector.tensor_tensor(a2[i // PACK][:, i % PACK, :], kept[i][:], entry[i][:], ALU.max)
 
         def interleave(copy, grouped, planar, cols):
             copy(
@@ -208,7 +217,7 @@ def tile_list_provenance_chain_features_kernel(
                 planar[:, :, cols].rearrange("p t (c e) -> p c t e", e=4),
             )
 
-        a2_codes = [keep.tile([P, KEPT], U32, name="a2_codes%d" % b, align_bytes=64) for b in range(PASSES)]
+        a2_codes = []
         a2_plane = [keep.tile([P, KEPT], U8, name="a2_plane%d" % b, align_bytes=64) for b in range(PASSES)]
 
         def quantize(codes, plane, grouped):
@@ -219,7 +228,7 @@ def tile_list_provenance_chain_features_kernel(
                 nc.tensor.matmul_mx(
                     out=banks[i][:],
                     lhsT=w4_codes[:, a, 2 * P * i : 2 * P * (i + 1)].bitcast(FP4X4),
-                    lhsT_scale=w4_plane[:, a, P * i : P * (i + 1)],
+                    lhsT_scale=w4_plane[:, i // PACK, a, P * (i % PACK) : P * (i % PACK + 1)],
                     rhs=a2_codes[a][:].bitcast(FP8X4),
                     rhs_scale=a2_plane[a][:],
                     start=(a == 0),
@@ -227,38 +236,51 @@ def tile_list_provenance_chain_features_kernel(
                 )
 
         first_stage(0)
-        quantize_w1(0, 0, 1)
-        quantize_w1(1, 0, 1, room=spare[2])
-        w4_plane = keep.tile([P, PASSES, H], U8, name="w4_plane", align_bytes=64)
+        quantize_w1(0, 0, 1, round_w1(0, 0, 1))
+        quantize_w1(1, 0, 1, round_w1(1, 0, 1, room=spare[1]))
+        w4_rows_dealt = keep.tile([P, PASS], U8, name="w4_rows_dealt", align_bytes=64)
         nc.vector.tensor_copy(
-            w4_plane[:].rearrange("p a (b t q) -> p (a b) t q", t=PACK, q=P),
-            w4_plane_raw[:].rearrange("p a (b q t) -> p (a b) t q", t=PACK, q=P),
+            w4_rows_dealt[:].rearrange("p (t q) -> p t q", t=PACK), w4_rows[:].rearrange("p (q t) -> p t q", t=PACK)
         )
+        for quad in range(4):
+            nc.sync.dma_start(
+                w4_plane[32 * quad : 32 * quad + 4].rearrange("r b a n -> r (b a) n").bitcast(I32),
+                w4_rows_dealt[32 * quad : 32 * quad + 16, :].bitcast(I32),
+            )
         pick_second(0)
-        pick_entry(0)
         pick_first_minus_second(0)
         times_link(0)
+        first_stage(1)
+        pick_second(1)
 
         everything = slice(0, KEPT)
-        for i in range(TILES - 1):
-            first_stage(i + 1)
-            if i < 2:
-                quantize_w1(0, 1, i)
-                quantize_w1(1, 1, i)
-            if i == TILES - 2:
-                w4_codes = keep.tile([P, PASSES, 2 * H], U8, name="w4_codes", align_bytes=64)
-                nc.scalar.copy(
-                    w4_codes[:].bitcast(U16).rearrange("p a (b t q) -> p (a b) t q", t=PACK, q=P),
-                    w4_raw[:].bitcast(U16).rearrange("p a (b q t) -> p (a b) t q", t=PACK, q=P),
-                )
-                grouped = ring.tile([P, KEPT, PACK], BF16, name="grouped", tag="grouped", bufs=2, align_bytes=64)
-                interleave(nc.scalar.copy, grouped, a2[0], everything)
-            pick_second(i + 1)
-            pick_kept(i)
+        for i in range(TILES - 2):
             pick_first_minus_second(i + 1)
-            larger(i)
             times_link(i + 1)
-            pick_entry(i + 1)
+            pick_kept(i)
+            pick_entry(i)
+            if i < 2:
+                rounded = [round_w1(a, 1, i) for a in range(PASSES)]
+            first_stage(i + 2)
+            if i < 2:
+                for a in range(PASSES):
+                    quantize_w1(a, 1, i, rounded[a])
+            pick_second(i + 2)
+            larger(i)
+        w4_codes = keep.tile([P, PASSES, 2 * H], U8, name="w4_codes", align_bytes=64)
+        nc.scalar.copy(
+            w4_codes[:].bitcast(U16).rearrange("p a (b t q) -> p (a b) t q", t=PACK, q=P),
+            w4_raw[:].bitcast(U16).rearrange("p a (b q t) -> p (a b) t q", t=PACK, q=P),
+        )
+        grouped = ring.tile([P, KEPT, PACK], BF16, name="grouped", tag="grouped", bufs=2, align_bytes=64)
+        interleave(nc.scalar.copy, grouped, a2[0], everything)
+        pick_first_minus_second(TILES - 1)
+        times_link(TILES - 1)
+        pick_kept(TILES - 2)
+        pick_entry(TILES - 2)
+        pick_entry(TILES - 1)
+        larger(TILES - 2)
+        a2_codes.append(keep.tile([P, KEPT], U32, name="a2_codes0", tag="diff", align_bytes=64))
         quantize(a2_codes[0][:], a2_plane[0][:], grouped)
         second_stage_pass(0)
         pick_kept(TILES - 1)
@@ -267,6 +289,7 @@ def tile_list_provenance_chain_features_kernel(
         grouped = ring.tile([P, KEPT, PACK], BF16, name="grouped", tag="grouped", bufs=2, align_bytes=64)
         interleave(nc.scalar.copy, grouped, a2[1], slice(0, 192))
         interleave(nc.vector.tensor_copy, grouped, a2[1], slice(192, KEPT))
+        a2_codes.append(keep.tile([P, KEPT], U32, name="a2_codes1", align_bytes=64))
         quantize(a2_codes[1][:], a2_plane[1][:], grouped)
         second_stage_pass(1)
 

@@ -24,6 +24,9 @@ BANK = 512
 CHUNKS = S // BANK
 TILES = H // P
 HELD = 4
+FUSED = 384
+PLAIN = PAIRS - FUSED
+HALF = KEPT // 2
 
 
 def tile_list_provenance_chain_features_kernel(
@@ -111,8 +114,8 @@ def tile_list_provenance_chain_features_kernel(
 
         def round_w1(a, b, u, pieces=1, room=None):
             if room is None:
-                room = ring.tile([P, BANK], F32, name="w1_grouped", tag="w1_grouped", bufs=3, align_bytes=64)
-            grouped = room[:].bitcast(BF16)
+                room = ring.tile([P, BANK], F32, name="w1_grouped", tag="w1_grouped", bufs=3, align_bytes=64)[:]
+            grouped = room.bitcast(BF16)
             for piece in range(pieces):
                 qs = slice(piece * P // pieces, (piece + 1) * P // pieces)
                 nc.scalar.copy(
@@ -121,11 +124,11 @@ def tile_list_provenance_chain_features_kernel(
                 )
             return grouped
 
-        def quantize_w1(a, b, u, grouped):
-            tag = "late%d%d" % (a, u) if b == 1 else "early%d%d" % (a, u)
-            codes = keep.tile([P, 2 * P], U32, name="w1_codes", tag=tag, align_bytes=64)
+        def quantize_w1(a, b, u, grouped, codes=None):
+            if codes is None:
+                codes = keep.tile([P, 2 * P], U32, name="w1_codes%d%d" % (a, u), align_bytes=64)[:]
             plane = keep.tile([P, 2 * P], U8, name="w1_plane%d%d%d" % (a, b, u), align_bytes=64)
-            nc.vector.quantize_mx(out=codes[:].bitcast(FP8X4), scales=plane[:], in_=grouped)
+            nc.vector.quantize_mx(out=codes.bitcast(FP8X4), scales=plane[:], in_=grouped)
             w1_codes[(a, b, u)] = codes
             w1_plane[(a, b, u)] = plane
 
@@ -139,7 +142,7 @@ def tile_list_provenance_chain_features_kernel(
         for c in range(CHUNKS - 1):
             pick_words_of_pass_1(c, keep.tile([P, BANK], U32, name="got_w1_%d" % c, align_bytes=64))
         first_room = keep.tile([P, BANK], F32, name="first_room", tag="handover", align_bytes=64)
-        quantize_w1(1, 0, 0, round_w1(1, 0, 0, pieces=2, room=first_room))
+        quantize_w1(1, 0, 0, round_w1(1, 0, 0, pieces=2, room=first_room[:]))
         pick_words_of_pass_1(CHUNKS - 1, keep.tile([P, BANK], U32, name="got_w1_last", tag="handover", align_bytes=64))
 
         link_sb = [load_link(0)]
@@ -150,7 +153,8 @@ def tile_list_provenance_chain_features_kernel(
         link_sb.append(load_link(1))
 
         spare = [keep.tile([P, BANK], F32, name="spare%d" % n, align_bytes=64) for n in range(CHUNKS)]
-        a2 = [keep.tile([P, PACK, KEPT], F32, name="a2_%d" % b) for b in range(PASSES)]
+        a2 = [keep.tile([P, PACK, KEPT], F32, name="a2_%d" % b, align_bytes=64) for b in range(PASSES)]
+        kept = [keep.tile([P, KEPT], F32, name="kept")] * (TILES - 1) + [spare[2]]
         h = []
 
         def first_stage(i):
@@ -173,10 +177,12 @@ def tile_list_provenance_chain_features_kernel(
                     )
                 if i == 0:
                     curved = spare[c][:]
-                elif i >= 2 and c == CHUNKS - 1:
+                elif i == 1 and c == CHUNKS - 1:
+                    curved = kept[0][:]
+                elif i in (2, 3, TILES - 1) and c == CHUNKS - 1:
+                    curved = keep.tile([P, BANK], F32, name="curved", tag="late%d" % (i - 2), align_bytes=64)[:]
+                elif c == CHUNKS - 1:
                     curved = a2[(i - 2) // PACK][:, (i - 2) % PACK, :]
-                elif i in (2, 3) and c in (1, 2):
-                    curved = keep.tile([P, BANK], F32, name="curved", tag="late%d%d" % (c - 1, i - 2), align_bytes=64)[:]
                 else:
                     curved = ring.tile([P, BANK], F32, name="curved", tag="curved", bufs=2)[:]
                 nc.scalar.activation(curved, bank[:], ACT.Gelu_apprx_tanh)
@@ -186,58 +192,79 @@ def tile_list_provenance_chain_features_kernel(
                     nc.scalar.activation(h_i[:, chunk], curved, ACT.Copy, scale=gain_sb[:, i : i + 1])
             h.append(h_i)
 
-        second = keep.tile([P, PAIRS], F32, name="second")
-        diff = keep.tile([P, PAIRS], F32, name="diff", tag="diff", align_bytes=64)
-        kept = [keep.tile([P, KEPT], F32, name="kept")] * (TILES - 1) + [spare[2]]
+        first = keep.tile([P, PLAIN], F32, name="first")
         entry = [keep.tile([P, KEPT], F32, name="entry")] * (TILES - 1) + [spare[0]]
-        a1 = []
+        second, diff, a1 = [], [], []
 
-        def pick_second(i):
-            nc.vector.tensor_copy(second[:], h[i][:].indirect(p2[:]))
+        def pick_plainly(i):
+            second.append(ring.tile([P, PAIRS], F32, name="second", tag="second", bufs=2))
+            if i == TILES - 1:
+                diff.append(keep.tile([P, PAIRS], F32, name="diff", tag="last_diff", align_bytes=64))
+                nc.vector.tensor_copy(second[i][:], h[i][:].indirect(p2[:]))
+                return
+            diff.append(ring.tile([P, PAIRS], F32, name="diff", tag="diff", bufs=2))
+            nc.vector.tensor_copy(second[i][:, :PLAIN], h[i][:].indirect(p2[:, : PLAIN // 16]))
+            nc.vector.tensor_copy(first[:], h[i][:].indirect(p1[:, : PLAIN // 16]))
+            nc.vector.tensor_copy(diff[i][:, :FUSED], h[i][:].indirect(p2[:, PLAIN // 16 :]))
 
-        def pick_first_minus_second(i):
-            nc.vector.tensor_tensor(diff[:], h[i][:].indirect(p1[:]), second[:], ALU.subtract)
+        def subtract(i):
+            if i == TILES - 1:
+                nc.vector.tensor_tensor(diff[i][:], h[i][:].indirect(p1[:]), second[i][:], ALU.subtract)
+                return
+            nc.vector.tensor_tensor(
+                diff[i][:, PLAIN:], h[i][:].indirect(p1[:, PLAIN // 16 :]), diff[i][:, :FUSED], ALU.subtract
+            )
+            nc.gpsimd.tensor_tensor(diff[i][:, :PLAIN], first[:], second[i][:, :PLAIN], ALU.subtract)
 
         def times_link(i):
             a1.append(ring.tile([P, PAIRS], F32, name="a1", tag="a1", bufs=2))
-            nc.gpsimd.tensor_tensor(a1[i][:], diff[:], link_sb[i // PACK][:, i % PACK, :], ALU.mult)
+            nc.gpsimd.tensor_tensor(a1[i][:], diff[i][:], link_sb[i // PACK][:, i % PACK, :], ALU.mult)
 
         def pick_entry(i):
             nc.vector.tensor_copy(entry[i][:], h[i][:].indirect(p4[:]))
 
-        def pick_kept(i):
-            nc.vector.tensor_copy(kept[i][:], a1[i][:].indirect(p3[:]))
+        def pick_kept(i, cols=slice(0, KEPT)):
+            nc.vector.tensor_copy(kept[i][:, cols], a1[i][:].indirect(p3[:, cols.start // 16 : cols.stop // 16]))
 
-        def larger(i):
-            nc.vector.tensor_tensor(a2[i // PACK][:, i % PACK, :], kept[i][:], entry[i][:], ALU.max)
+        def larger(i, cols=slice(0, KEPT)):
+            nc.vector.tensor_tensor(a2[i // PACK][:, i % PACK, cols], kept[i][:, cols], entry[i][:, cols], ALU.max)
 
-        def interleave(copy, grouped, planar, cols):
-            copy(
-                grouped[:, cols, :].rearrange("p (c e) t -> p c t e", e=4),
-                planar[:, :, cols].rearrange("p t (c e) -> p c t e", e=4),
-            )
+        halves = [slice(half * HALF, (half + 1) * HALF) for half in range(2)]
 
-        a2_codes = []
-        a2_plane = [keep.tile([P, KEPT], U8, name="a2_plane%d" % b, align_bytes=64) for b in range(PASSES)]
+        def interleave(copy, planar, room=None):
+            if room is None:
+                room = ring.tile([P, BANK], F32, name="grouped", tag="grouped", bufs=4, align_bytes=64)[:]
+            grouped = room.bitcast(BF16)
+            copy(grouped.rearrange("p (c e t) -> p c t e", e=4, t=PACK), planar.rearrange("p t (c e) -> p c t e", e=4))
+            return grouped
 
         def quantize(codes, plane, grouped):
-            nc.vector.quantize_mx(out=codes.bitcast(FP8X4), scales=plane, in_=grouped[:].rearrange("p m t -> p (m t)"))
+            nc.vector.quantize_mx(out=codes.bitcast(FP8X4), scales=plane, in_=grouped)
 
-        def second_stage_pass(a):
+        def sums(i, half):
+            return banks[PACK * half + i // 2][:, halves[i % 2]]
+
+        def second_stage_pass(a, half, codes, plane):
             for i in range(TILES):
                 nc.tensor.matmul_mx(
-                    out=banks[i][:],
+                    out=sums(i, half),
                     lhsT=w4_codes[:, a, 2 * P * i : 2 * P * (i + 1)].bitcast(FP4X4),
                     lhsT_scale=w4_plane[:, i // PACK, a, P * (i % PACK) : P * (i % PACK + 1)],
-                    rhs=a2_codes[a][:].bitcast(FP8X4),
-                    rhs_scale=a2_plane[a][:],
-                    start=(a == 0),
-                    stop=(a == PASSES - 1),
+                    rhs=codes.bitcast(FP8X4),
+                    rhs_scale=plane,
+                    start=(a == 0 and i % 2 == 0),
+                    stop=(a == PASSES - 1 and i % 2 == 1),
                 )
+
+        def quantize_and_multiply(a, half, grouped, tag):
+            codes = keep.tile([P, HALF], U32, name="a2_codes", tag=tag, align_bytes=64)
+            plane = keep.tile([P, HALF], U8, name="a2_plane%d%d" % (a, half), align_bytes=64)
+            quantize(codes[:], plane[:], grouped)
+            second_stage_pass(a, half, codes[:], plane[:])
 
         first_stage(0)
         quantize_w1(0, 0, 1, round_w1(0, 0, 1))
-        quantize_w1(1, 0, 1, round_w1(1, 0, 1, room=spare[1]))
+        quantize_w1(1, 0, 1, round_w1(1, 0, 1, room=spare[1][:]))
         w4_rows_dealt = keep.tile([P, PASS], U8, name="w4_rows_dealt", align_bytes=64)
         nc.vector.tensor_copy(
             w4_rows_dealt[:].rearrange("p (t q) -> p t q", t=PACK), w4_rows[:].rearrange("p (q t) -> p t q", t=PACK)
@@ -247,69 +274,76 @@ def tile_list_provenance_chain_features_kernel(
                 w4_plane[32 * quad : 32 * quad + 4].rearrange("r b a n -> r (b a) n").bitcast(I32),
                 w4_rows_dealt[32 * quad : 32 * quad + 16, :].bitcast(I32),
             )
-        pick_second(0)
-        pick_first_minus_second(0)
+        pick_plainly(0)
+        subtract(0)
         times_link(0)
         first_stage(1)
-        pick_second(1)
+        pick_plainly(1)
 
-        everything = slice(0, KEPT)
         for i in range(TILES - 2):
-            pick_first_minus_second(i + 1)
+            subtract(i + 1)
             times_link(i + 1)
             pick_kept(i)
             pick_entry(i)
             if i < 2:
-                rounded = [round_w1(a, 1, i) for a in range(PASSES)]
+                rounded = [round_w1(0, 1, i, room=a2[0][:, i, :]), round_w1(1, 1, i)]
+            if i == TILES - 4:
+                w4_codes = keep.tile([P, PASSES, 2 * H], U8, name="w4_codes", align_bytes=64)
+                nc.scalar.copy(
+                    w4_codes[:].bitcast(U16).rearrange("p a (b t q) -> p (a b) t q", t=PACK, q=P),
+                    w4_raw[:].bitcast(U16).rearrange("p a (b q t) -> p (a b) t q", t=PACK, q=P),
+                )
+            if i == TILES - 3:
+                grouped = [interleave(nc.scalar.copy, a2[0][:, :, halves[0]], room=a2[1][:, 1, :])]
             first_stage(i + 2)
+            pick_plainly(i + 2)
             if i < 2:
+                codes = keep.tile([P, PASSES, 2 * P], U32, name="w1_codes", tag="late%d" % i, align_bytes=64)
                 for a in range(PASSES):
-                    quantize_w1(a, 1, i, rounded[a])
-            pick_second(i + 2)
+                    quantize_w1(a, 1, i, rounded[a], codes[:, a, :])
+            if i == TILES - 3:
+                quantize_and_multiply(0, 0, grouped[0], "late%d" % i)
             larger(i)
-        w4_codes = keep.tile([P, PASSES, 2 * H], U8, name="w4_codes", align_bytes=64)
-        nc.scalar.copy(
-            w4_codes[:].bitcast(U16).rearrange("p a (b t q) -> p (a b) t q", t=PACK, q=P),
-            w4_raw[:].bitcast(U16).rearrange("p a (b q t) -> p (a b) t q", t=PACK, q=P),
-        )
-        grouped = ring.tile([P, KEPT, PACK], BF16, name="grouped", tag="grouped", bufs=2, align_bytes=64)
-        interleave(nc.scalar.copy, grouped, a2[0], everything)
-        pick_first_minus_second(TILES - 1)
+        grouped.append(interleave(nc.scalar.copy, a2[0][:, :, halves[1]]))
+        subtract(TILES - 1)
         times_link(TILES - 1)
         pick_kept(TILES - 2)
         pick_entry(TILES - 2)
         pick_entry(TILES - 1)
         larger(TILES - 2)
-        a2_codes.append(keep.tile([P, KEPT], U32, name="a2_codes0", tag="diff", align_bytes=64))
-        quantize(a2_codes[0][:], a2_plane[0][:], grouped)
-        second_stage_pass(0)
-        pick_kept(TILES - 1)
-        larger(TILES - 1)
+        quantize_and_multiply(0, 1, grouped[1], "last_diff")
+        for half in range(2):
+            pick_kept(TILES - 1, halves[half])
+        for half in range(2):
+            larger(TILES - 1, halves[half])
+        grouped = [
+            interleave(nc.scalar.copy, a2[1][:, :, halves[0]]),
+            interleave(nc.vector.tensor_copy, a2[1][:, :, halves[1]]),
+        ]
+        for half in range(2):
+            quantize_and_multiply(1, half, grouped[half], "a2_codes1%d" % half)
 
-        grouped = ring.tile([P, KEPT, PACK], BF16, name="grouped", tag="grouped", bufs=2, align_bytes=64)
-        interleave(nc.scalar.copy, grouped, a2[1], slice(0, 192))
-        interleave(nc.vector.tensor_copy, grouped, a2[1], slice(192, KEPT))
-        a2_codes.append(keep.tile([P, KEPT], U32, name="a2_codes1", align_bytes=64))
-        quantize(a2_codes[1][:], a2_plane[1][:], grouped)
-        second_stage_pass(1)
-
-        y = [ring.tile([P, PACK, KEPT], F32, name="y%d" % b, tag="rows", bufs=4, align_bytes=64) for b in range(PASSES)]
-        y_codes = [keep.tile([P, KEPT], U32, name="y_codes%d" % b, align_bytes=64) for b in range(PASSES)]
         y_plane = keep.tile([P, PASSES, KEPT], U8, name="y_plane", align_bytes=64)
-        y_grouped = []
-        for b in range(PASSES):
-            rows = out_0[b * PASS : (b + 1) * PASS, :].rearrange("(p t) j -> p t j", t=PACK)
-            for t in range(PACK):
-                i = PACK * b + t
-                nc.vector.scalar_tensor_tensor(
-                    y[b][:, t, :], a2[b][:, t, :], skip_sb[:, i : i + 1], banks[i][:], ALU.mult, ALU.add
-                )
-                nc.sync.dma_start(rows[:, t, :], y[b][:, t, :])
-            y_grouped.append(ring.tile([P, KEPT, PACK], BF16, name="grouped", tag="grouped", bufs=2, align_bytes=64))
-            interleave(nc.scalar.copy if b == 0 else nc.vector.tensor_copy, y_grouped[b], y[b], everything)
-        for b in range(PASSES):
-            quantize(y_codes[b][:], y_plane[:, b, :], y_grouped[b])
-            nc.sync.dma_start(out_1[b].rearrange("p m t -> p (m t)").bitcast(I32), y_codes[b][:].bitcast(I32))
+        y_grouped = {}
+        for half in range(2):
+            for b in range(PASSES):
+                y = ring.tile([P, PACK, HALF], F32, name="y", tag="rows", bufs=4, align_bytes=64)
+                rows = out_0[b * PASS : (b + 1) * PASS, halves[half]].rearrange("(p t) j -> p t j", t=PACK)
+                for t in range(PACK):
+                    i = PACK * b + t
+                    nc.vector.scalar_tensor_tensor(
+                        y[:, t, :], a2[b][:, t, halves[half]], skip_sb[:, i : i + 1], sums(i, half), ALU.mult, ALU.add
+                    )
+                    if t % 2:
+                        nc.sync.dma_start(rows[:, t - 1 : t + 1, :], y[:, t - 1 : t + 1, :])
+                last = half == 1 and b == PASSES - 1
+                y_grouped[(half, b)] = interleave(nc.vector.tensor_copy if last else nc.scalar.copy, y[:])
+        for half in range(2):
+            for b in range(PASSES):
+                codes = keep.tile([P, HALF], U32, name="y_codes%d%d" % (half, b), align_bytes=64)
+                quantize(codes[:], y_plane[:, b, halves[half]], y_grouped[(half, b)])
+                words = out_1[b].rearrange("p m t -> p (m t)").bitcast(I32)
+                nc.sync.dma_start(words[:, halves[half]], codes[:].bitcast(I32))
         for quad in range(4):
             queue = nc.scalar if quad % 2 else nc.sync
             queue.dma_start(

@@ -21,12 +21,17 @@ PACK = 4
 PASS = P * PACK
 PASSES = 2
 BANK = 512
+BANKS = 8
+QUADRANTS = 4
+STRIPE = 16
 CHUNKS = S // BANK
 TILES = H // P
-HELD = 4
-FUSED = 384
-PLAIN = PAIRS - FUSED
+LAST = TILES - 1
+H_AHEAD = 4
 HALF = KEPT // 2
+W1_STEPS = (0, 2)
+W4_STEP = TILES - 4
+FIRST_HALF_STEP = TILES - 3
 
 
 def tile_list_provenance_chain_features_kernel(
@@ -46,19 +51,19 @@ def tile_list_provenance_chain_features_kernel(
 
         def load_table_words(a):
             tile = ring.tile([P, T], U32, name="tab_words%d" % a, tag="wide", bufs=2, align_bytes=64)
-            words = tab_words[a].rearrange("p t i -> p (t i)").bitcast(I32)
-            for half in range(2):
-                cols = slice(half * T // 2, (half + 1) * T // 2)
-                nc.sync.dma_start(tile[:].bitcast(I32)[:, cols], words[:, cols])
+            source = tab_words[a].rearrange("p t i -> p (t i)").bitcast(I32)
+            for part in range(2):
+                cols = slice(part * T // 2, (part + 1) * T // 2)
+                nc.sync.dma_start(tile[:].bitcast(I32)[:, cols], source[:, cols])
             return tile
 
         def load_w1(a, b, pieces=1):
             tile = ring.tile([P, PACK, PASS], F32, name="w1_%d%d" % (a, b), tag="rows", bufs=4, align_bytes=64)
-            rows = w1[a * PASS : (a + 1) * PASS, b * PASS : (b + 1) * PASS]
-            rows = rows.rearrange("(p j) n -> p j n", j=PACK)
+            source = w1[a * PASS : (a + 1) * PASS, b * PASS : (b + 1) * PASS]
+            source = source.rearrange("(p j) n -> p j n", j=PACK)
             for piece in range(pieces):
                 cols = slice(piece * PASS // pieces, (piece + 1) * PASS // pieces)
-                nc.sync.dma_start(tile[:, :, cols], rows[:, :, cols])
+                nc.sync.dma_start(tile[:, :, cols], source[:, :, cols])
             return tile
 
         def load_per_row(name, source):
@@ -68,15 +73,14 @@ def tile_list_provenance_chain_features_kernel(
             )
             return tile
 
-        def load_link(b):
-            tile = ring.tile([P, PACK, PAIRS], F32, name="link%d" % b, tag="wide", bufs=2, align_bytes=64)
-            nc.sync.dma_start(tile[:], link[b * PASS : (b + 1) * PASS, :].rearrange("(p t) m -> p t m", t=PACK))
-            return tile
+        def load_link(tile, b, ts):
+            source = link[b * PASS : (b + 1) * PASS, :].rearrange("(p t) m -> p t m", t=PACK)
+            nc.sync.dma_start(tile[:, ts, :], source[:, ts, :])
 
         tab_plane = keep.tile([P, T], U8, name="tab_plane", align_bytes=64)
         nc.vector.memset(tab_plane[:].bitcast(I32)[:, : T // 8], 0)
         nc.gpsimd.memset(tab_plane[:].bitcast(I32)[:, T // 8 :], 0)
-        for quad in range(4):
+        for quad in range(QUADRANTS):
             nc.sync.dma_start(
                 tab_plane[32 * quad : 32 * quad + 8, :].bitcast(I32),
                 tab_scales[:, 4 * quad : 4 * quad + 4, :].bitcast(I32),
@@ -88,22 +92,22 @@ def tile_list_provenance_chain_features_kernel(
 
         idx = load_list("idx", offs)
         gain_sb = load_per_row("gain_sb", gain)
-        p2 = load_list("p2", pos2)
-        p4 = load_list("p4", pos4)
         tab_w = [load_table_words(0)]
-        p1 = load_list("p1", pos1)
-        p3 = load_list("p3", pos3)
-        skip_sb = load_per_row("skip_sb", skip)
         w1_raw = {(0, 0): load_w1(0, 0)}
         tab_w.append(load_table_words(1))
         w1_raw[(1, 0)] = load_w1(1, 0, pieces=2)
-        for quad in range(4):
+        p2 = load_list("p2", pos2)
+        p4 = load_list("p4", pos4)
+        p1 = load_list("p1", pos1)
+        p3 = load_list("p3", pos3)
+        skip_sb = load_per_row("skip_sb", skip)
+        for quad in range(QUADRANTS):
             nc.sync.dma_start(
                 w4_rows[32 * quad : 32 * quad + 16, :].bitcast(I32),
                 w4_scales[:, 4 * quad : 4 * quad + 4, :].rearrange("a r (b n) -> (r b) a n", n=PASS).bitcast(I32),
             )
 
-        banks = [psum.tile([P, BANK], F32, name="bank%d" % n) for n in range(8)]
+        banks = [psum.tile([P, BANK], F32, name="bank%d" % n) for n in range(BANKS)]
 
         got_w0 = keep.tile([P, S], U32, name="got_w0", align_bytes=64)
         nc.vector.tensor_copy(got_w0[:], tab_w[0][:].indirect(idx[:]))
@@ -114,28 +118,29 @@ def tile_list_provenance_chain_features_kernel(
 
         def round_w1(a, b, u, pieces=1, room=None):
             if room is None:
-                room = ring.tile([P, BANK], F32, name="w1_grouped", tag="w1_grouped", bufs=3, align_bytes=64)[:]
-            grouped = room.bitcast(BF16)
+                room = ring.tile([P, BANK], F32, name="w1_room", tag="w1_room", bufs=3, align_bytes=64)[:]
+            rounded = room.bitcast(BF16)
             for piece in range(pieces):
                 qs = slice(piece * P // pieces, (piece + 1) * P // pieces)
                 nc.scalar.copy(
-                    grouped.rearrange("p (t q j) -> p q j t", t=2, j=PACK)[:, qs],
+                    rounded.rearrange("p (t q j) -> p q j t", t=2, j=PACK)[:, qs],
                     w1_raw[(a, b)][:].rearrange("p j (q t) -> p q j t", t=PACK)[:, qs, :, 2 * u : 2 * u + 2],
                 )
-            return grouped
+            return rounded
 
-        def quantize_w1(a, b, u, grouped, codes=None):
+        def quantize_w1(a, b, u, rounded, codes=None):
             if codes is None:
                 codes = keep.tile([P, 2 * P], U32, name="w1_codes%d%d" % (a, u), align_bytes=64)[:]
             plane = keep.tile([P, 2 * P], U8, name="w1_plane%d%d%d" % (a, b, u), align_bytes=64)
-            nc.vector.quantize_mx(out=codes.bitcast(FP8X4), scales=plane[:], in_=grouped)
+            nc.vector.quantize_mx(out=codes.bitcast(FP8X4), scales=plane[:], in_=rounded)
             w1_codes[(a, b, u)] = codes
             w1_plane[(a, b, u)] = plane
 
         got_w1 = []
 
         def pick_words_of_pass_1(c, tile):
-            nc.vector.tensor_copy(tile[:], tab_w[1][:].indirect(idx[:, c * (BANK // 16) : (c + 1) * (BANK // 16)]))
+            entries = idx[:, c * (BANK // STRIPE) : (c + 1) * (BANK // STRIPE)]
+            nc.vector.tensor_copy(tile[:], tab_w[1][:].indirect(entries))
             got_w1.append(tile)
 
         quantize_w1(0, 0, 0, round_w1(0, 0, 0))
@@ -145,46 +150,52 @@ def tile_list_provenance_chain_features_kernel(
         quantize_w1(1, 0, 0, round_w1(1, 0, 0, pieces=2, room=first_room[:]))
         pick_words_of_pass_1(CHUNKS - 1, keep.tile([P, BANK], U32, name="got_w1_last", tag="handover", align_bytes=64))
 
-        link_sb = [load_link(0)]
+        link_sb = [
+            ring.tile([P, PACK, PAIRS], F32, name="link%d" % b, tag="wide", bufs=2, align_bytes=64) for b in range(PASSES)
+        ]
+        load_link(link_sb[0], 0, slice(0, 2))
         w1_raw[(0, 1)] = load_w1(0, 1)
         w1_raw[(1, 1)] = load_w1(1, 1)
+        load_link(link_sb[0], 0, slice(2, PACK))
         w4_raw = keep.tile([P, PASSES, 2 * H], U8, name="w4_raw", align_bytes=64)
         nc.sync.dma_start(w4_raw[:].bitcast(I32), w4_words.rearrange("a p n -> p a n").bitcast(I32))
-        link_sb.append(load_link(1))
+        load_link(link_sb[1], 1, slice(0, PACK))
 
         spare = [keep.tile([P, BANK], F32, name="spare%d" % n, align_bytes=64) for n in range(CHUNKS)]
         a2 = [keep.tile([P, PACK, KEPT], F32, name="a2_%d" % b, align_bytes=64) for b in range(PASSES)]
-        kept = [keep.tile([P, KEPT], F32, name="kept")] * (TILES - 1) + [spare[2]]
+        kept = [keep.tile([P, KEPT], F32, name="kept")] * LAST + [spare[2]]
         h = []
+
+        def gelu_buffer(i, c):
+            if i == 0:
+                return spare[c][:]
+            if c < CHUNKS - 1:
+                return ring.tile([P, BANK], F32, name="curved", tag="curved", bufs=2)[:]
+            if i == 1:
+                return kept[0][:]
+            if i - 2 in W1_STEPS or i - 2 == FIRST_HALF_STEP:
+                return keep.tile([P, BANK], F32, name="curved", tag="step%d" % (i - 2), align_bytes=64)[:]
+            return a2[(i - 2) // PACK][:, (i - 2) % PACK, :]
 
         def first_stage(i):
             b, t = divmod(i, PACK)
             u, cols = t // 2, slice((t % 2) * P, (t % 2 + 1) * P)
-            h_i = ring.tile([P, S], F32, name="h", tag="h", bufs=HELD)
+            h_i = ring.tile([P, S], F32, name="h", tag="h", bufs=H_AHEAD)
             for c in range(CHUNKS):
-                bank = banks[(CHUNKS * i + c) % 8]
+                bank = banks[(CHUNKS * i + c) % BANKS]
                 chunk = slice(c * BANK, (c + 1) * BANK)
                 for a in range(PASSES):
-                    words = got_w0[:, chunk] if a == 0 else got_w1[c][:]
+                    moving = got_w0[:, chunk] if a == 0 else got_w1[c][:]
                     nc.tensor.matmul_mx(
                         out=bank[:],
                         lhsT=w1_codes[(a, b, u)][:, cols].bitcast(FP8X4),
                         lhsT_scale=w1_plane[(a, b, u)][:, cols],
-                        rhs=words.bitcast(FP8X4),
+                        rhs=moving.bitcast(FP8X4),
                         rhs_scale=got_plane[4 * a : P, chunk],
                         start=(a == 0),
                         stop=(a == PASSES - 1),
                     )
-                if i == 0:
-                    curved = spare[c][:]
-                elif i == 1 and c == CHUNKS - 1:
-                    curved = kept[0][:]
-                elif i in (2, 3, TILES - 1) and c == CHUNKS - 1:
-                    curved = keep.tile([P, BANK], F32, name="curved", tag="late%d" % (i - 2), align_bytes=64)[:]
-                elif c == CHUNKS - 1:
-                    curved = a2[(i - 2) // PACK][:, (i - 2) % PACK, :]
-                else:
-                    curved = ring.tile([P, BANK], F32, name="curved", tag="curved", bufs=2)[:]
+                curved = gelu_buffer(i, c)
                 nc.scalar.activation(curved, bank[:], ACT.Gelu_apprx_tanh)
                 if i == 0:
                     nc.vector.tensor_scalar(h_i[:, chunk], curved, gain_sb[:, 0:1], None, ALU.mult)
@@ -192,39 +203,27 @@ def tile_list_provenance_chain_features_kernel(
                     nc.scalar.activation(h_i[:, chunk], curved, ACT.Copy, scale=gain_sb[:, i : i + 1])
             h.append(h_i)
 
-        first = keep.tile([P, PLAIN], F32, name="first")
-        entry = [keep.tile([P, KEPT], F32, name="entry")] * (TILES - 1) + [spare[0]]
-        second, diff, a1 = [], [], []
+        second = keep.tile([P, PAIRS], F32, name="second")
+        diff = keep.tile([P, PAIRS], F32, name="diff", tag="diff", align_bytes=64)
+        entry = [keep.tile([P, KEPT], F32, name="entry")] * LAST + [spare[0]]
+        a1 = []
 
-        def pick_plainly(i):
-            second.append(ring.tile([P, PAIRS], F32, name="second", tag="second", bufs=2))
-            if i == TILES - 1:
-                diff.append(keep.tile([P, PAIRS], F32, name="diff", tag="last_diff", align_bytes=64))
-                nc.vector.tensor_copy(second[i][:], h[i][:].indirect(p2[:]))
-                return
-            diff.append(ring.tile([P, PAIRS], F32, name="diff", tag="diff", bufs=2))
-            nc.vector.tensor_copy(second[i][:, :PLAIN], h[i][:].indirect(p2[:, : PLAIN // 16]))
-            nc.vector.tensor_copy(first[:], h[i][:].indirect(p1[:, : PLAIN // 16]))
-            nc.vector.tensor_copy(diff[i][:, :FUSED], h[i][:].indirect(p2[:, PLAIN // 16 :]))
+        def pick_second(i):
+            nc.vector.tensor_copy(second[:], h[i][:].indirect(p2[:]))
 
         def subtract(i):
-            if i == TILES - 1:
-                nc.vector.tensor_tensor(diff[i][:], h[i][:].indirect(p1[:]), second[i][:], ALU.subtract)
-                return
-            nc.vector.tensor_tensor(
-                diff[i][:, PLAIN:], h[i][:].indirect(p1[:, PLAIN // 16 :]), diff[i][:, :FUSED], ALU.subtract
-            )
-            nc.gpsimd.tensor_tensor(diff[i][:, :PLAIN], first[:], second[i][:, :PLAIN], ALU.subtract)
+            nc.vector.tensor_tensor(diff[:], h[i][:].indirect(p1[:]), second[:], ALU.subtract)
 
         def times_link(i):
             a1.append(ring.tile([P, PAIRS], F32, name="a1", tag="a1", bufs=2))
-            nc.gpsimd.tensor_tensor(a1[i][:], diff[i][:], link_sb[i // PACK][:, i % PACK, :], ALU.mult)
+            nc.gpsimd.tensor_tensor(a1[i][:], diff[:], link_sb[i // PACK][:, i % PACK, :], ALU.mult)
 
         def pick_entry(i):
             nc.vector.tensor_copy(entry[i][:], h[i][:].indirect(p4[:]))
 
         def pick_kept(i, cols=slice(0, KEPT)):
-            nc.vector.tensor_copy(kept[i][:, cols], a1[i][:].indirect(p3[:, cols.start // 16 : cols.stop // 16]))
+            entries = p3[:, cols.start // STRIPE : cols.stop // STRIPE]
+            nc.vector.tensor_copy(kept[i][:, cols], a1[i][:].indirect(entries))
 
         def larger(i, cols=slice(0, KEPT)):
             nc.vector.tensor_tensor(a2[i // PACK][:, i % PACK, cols], kept[i][:, cols], entry[i][:, cols], ALU.max)
@@ -233,34 +232,31 @@ def tile_list_provenance_chain_features_kernel(
 
         def interleave(copy, planar, room=None):
             if room is None:
-                room = ring.tile([P, BANK], F32, name="grouped", tag="grouped", bufs=4, align_bytes=64)[:]
-            grouped = room.bitcast(BF16)
-            copy(grouped.rearrange("p (c e t) -> p c t e", e=4, t=PACK), planar.rearrange("p t (c e) -> p c t e", e=4))
-            return grouped
+                room = ring.tile([P, BANK], F32, name="room", tag="room", bufs=4, align_bytes=64)[:]
+            rounded = room.bitcast(BF16)
+            copy(rounded.rearrange("p (c e t) -> p c t e", e=4, t=PACK), planar.rearrange("p t (c e) -> p c t e", e=4))
+            return rounded
 
-        def quantize(codes, plane, grouped):
-            nc.vector.quantize_mx(out=codes.bitcast(FP8X4), scales=plane, in_=grouped)
+        def quantize(codes, plane, rounded):
+            nc.vector.quantize_mx(out=codes.bitcast(FP8X4), scales=plane, in_=rounded)
 
         def sums(i, half):
-            return banks[PACK * half + i // 2][:, halves[i % 2]]
+            return banks[(BANKS // 2) * half + i // 2][:, halves[i % 2]]
 
-        def second_stage_pass(a, half, codes, plane):
+        def quantize_and_multiply(a, half, rounded, tag):
+            codes = keep.tile([P, HALF], U32, name="a2_codes", tag=tag, align_bytes=64)
+            plane = keep.tile([P, HALF], U8, name="a2_plane%d%d" % (a, half), align_bytes=64)
+            quantize(codes[:], plane[:], rounded)
             for i in range(TILES):
                 nc.tensor.matmul_mx(
                     out=sums(i, half),
                     lhsT=w4_codes[:, a, 2 * P * i : 2 * P * (i + 1)].bitcast(FP4X4),
                     lhsT_scale=w4_plane[:, i // PACK, a, P * (i % PACK) : P * (i % PACK + 1)],
-                    rhs=codes.bitcast(FP8X4),
-                    rhs_scale=plane,
+                    rhs=codes[:].bitcast(FP8X4),
+                    rhs_scale=plane[:],
                     start=(a == 0 and i % 2 == 0),
                     stop=(a == PASSES - 1 and i % 2 == 1),
                 )
-
-        def quantize_and_multiply(a, half, grouped, tag):
-            codes = keep.tile([P, HALF], U32, name="a2_codes", tag=tag, align_bytes=64)
-            plane = keep.tile([P, HALF], U8, name="a2_plane%d%d" % (a, half), align_bytes=64)
-            quantize(codes[:], plane[:], grouped)
-            second_stage_pass(a, half, codes[:], plane[:])
 
         first_stage(0)
         quantize_w1(0, 0, 1, round_w1(0, 0, 1))
@@ -269,82 +265,83 @@ def tile_list_provenance_chain_features_kernel(
         nc.vector.tensor_copy(
             w4_rows_dealt[:].rearrange("p (t q) -> p t q", t=PACK), w4_rows[:].rearrange("p (q t) -> p t q", t=PACK)
         )
-        for quad in range(4):
+        for quad in range(QUADRANTS):
             nc.sync.dma_start(
                 w4_plane[32 * quad : 32 * quad + 4].rearrange("r b a n -> r (b a) n").bitcast(I32),
                 w4_rows_dealt[32 * quad : 32 * quad + 16, :].bitcast(I32),
             )
-        pick_plainly(0)
+        pick_second(0)
         subtract(0)
         times_link(0)
         first_stage(1)
-        pick_plainly(1)
+        pick_second(1)
 
         for i in range(TILES - 2):
             subtract(i + 1)
             times_link(i + 1)
             pick_kept(i)
             pick_entry(i)
-            if i < 2:
-                rounded = [round_w1(0, 1, i, room=a2[0][:, i, :]), round_w1(1, 1, i)]
-            if i == TILES - 4:
+            if i in W1_STEPS:
+                w1_rounded = [round_w1(0, 1, i // 2, room=a2[0][:, i, :]), round_w1(1, 1, i // 2)]
+            if i == W4_STEP:
                 w4_codes = keep.tile([P, PASSES, 2 * H], U8, name="w4_codes", align_bytes=64)
                 nc.scalar.copy(
                     w4_codes[:].bitcast(U16).rearrange("p a (b t q) -> p (a b) t q", t=PACK, q=P),
                     w4_raw[:].bitcast(U16).rearrange("p a (b q t) -> p (a b) t q", t=PACK, q=P),
                 )
-            if i == TILES - 3:
-                grouped = [interleave(nc.scalar.copy, a2[0][:, :, halves[0]], room=a2[1][:, 1, :])]
+            if i == FIRST_HALF_STEP:
+                first_half = interleave(nc.scalar.copy, a2[0][:, :, halves[0]], room=a2[1][:, i % PACK, :])
             first_stage(i + 2)
-            pick_plainly(i + 2)
-            if i < 2:
-                codes = keep.tile([P, PASSES, 2 * P], U32, name="w1_codes", tag="late%d" % i, align_bytes=64)
+            pick_second(i + 2)
+            if i in W1_STEPS:
+                codes = keep.tile([P, PASSES, 2 * P], U32, name="w1_codes", tag="step%d" % i, align_bytes=64)
                 for a in range(PASSES):
-                    quantize_w1(a, 1, i, rounded[a], codes[:, a, :])
-            if i == TILES - 3:
-                quantize_and_multiply(0, 0, grouped[0], "late%d" % i)
+                    quantize_w1(a, 1, i // 2, w1_rounded[a], codes[:, a, :])
+            if i == FIRST_HALF_STEP:
+                quantize_and_multiply(0, 0, first_half, "step%d" % i)
             larger(i)
-        grouped.append(interleave(nc.scalar.copy, a2[0][:, :, halves[1]]))
-        subtract(TILES - 1)
-        times_link(TILES - 1)
-        pick_kept(TILES - 2)
-        pick_entry(TILES - 2)
-        pick_entry(TILES - 1)
-        larger(TILES - 2)
-        quantize_and_multiply(0, 1, grouped[1], "last_diff")
+
+        second_half = interleave(nc.scalar.copy, a2[0][:, :, halves[1]])
+        subtract(LAST)
+        times_link(LAST)
+        pick_kept(LAST - 1)
+        pick_entry(LAST - 1)
+        pick_entry(LAST)
+        larger(LAST - 1)
+        quantize_and_multiply(0, 1, second_half, "diff")
         for half in range(2):
-            pick_kept(TILES - 1, halves[half])
+            pick_kept(LAST, halves[half])
         for half in range(2):
-            larger(TILES - 1, halves[half])
-        grouped = [
+            larger(LAST, halves[half])
+        a2_rounded = [
             interleave(nc.scalar.copy, a2[1][:, :, halves[0]]),
             interleave(nc.vector.tensor_copy, a2[1][:, :, halves[1]]),
         ]
         for half in range(2):
-            quantize_and_multiply(1, half, grouped[half], "a2_codes1%d" % half)
+            quantize_and_multiply(1, half, a2_rounded[half], "a2_codes1%d" % half)
 
         y_plane = keep.tile([P, PASSES, KEPT], U8, name="y_plane", align_bytes=64)
-        y_grouped = {}
+        y_rounded = {}
         for half in range(2):
             for b in range(PASSES):
                 y = ring.tile([P, PACK, HALF], F32, name="y", tag="rows", bufs=4, align_bytes=64)
-                rows = out_0[b * PASS : (b + 1) * PASS, halves[half]].rearrange("(p t) j -> p t j", t=PACK)
+                target = out_0[b * PASS : (b + 1) * PASS, halves[half]].rearrange("(p t) j -> p t j", t=PACK)
                 for t in range(PACK):
                     i = PACK * b + t
                     nc.vector.scalar_tensor_tensor(
                         y[:, t, :], a2[b][:, t, halves[half]], skip_sb[:, i : i + 1], sums(i, half), ALU.mult, ALU.add
                     )
                     if t % 2:
-                        nc.sync.dma_start(rows[:, t - 1 : t + 1, :], y[:, t - 1 : t + 1, :])
-                last = half == 1 and b == PASSES - 1
-                y_grouped[(half, b)] = interleave(nc.vector.tensor_copy if last else nc.scalar.copy, y[:])
+                        nc.sync.dma_start(target[:, t - 1 : t + 1, :], y[:, t - 1 : t + 1, :])
+                last_quarter = half == 1 and b == PASSES - 1
+                y_rounded[(half, b)] = interleave(nc.vector.tensor_copy if last_quarter else nc.scalar.copy, y[:])
         for half in range(2):
             for b in range(PASSES):
                 codes = keep.tile([P, HALF], U32, name="y_codes%d%d" % (half, b), align_bytes=64)
-                quantize(codes[:], y_plane[:, b, halves[half]], y_grouped[(half, b)])
-                words = out_1[b].rearrange("p m t -> p (m t)").bitcast(I32)
-                nc.sync.dma_start(words[:, halves[half]], codes[:].bitcast(I32))
-        for quad in range(4):
+                quantize(codes[:], y_plane[:, b, halves[half]], y_rounded[(half, b)])
+                y_words = out_1[b].rearrange("p m t -> p (m t)").bitcast(I32)
+                nc.sync.dma_start(y_words[:, halves[half]], codes[:].bitcast(I32))
+        for quad in range(QUADRANTS):
             queue = nc.scalar if quad % 2 else nc.sync
             queue.dma_start(
                 out_2[:, 4 * quad : 4 * quad + 4, :].rearrange("g r m -> r g m").bitcast(I32),

from contextlib import ExitStack

import concourse.mybir as mybir

K, H, T, S, PAIRS, KEPT = 1024, 1024, 4096, 2048, 1024, 512
FLOPS = 2 * K * H * S + 2 * H * H * KEPT

F32 = mybir.dt.float32
BF16 = mybir.dt.bfloat16
I32 = mybir.dt.int32
U32 = mybir.dt.uint32
U16 = mybir.dt.uint16
U8 = mybir.dt.uint8
FP8X4 = mybir.dt.float8_e4m3fn_x4
FP4X4 = mybir.dt.float4_e2m1fn_x4
ALU = mybir.AluOpType
ACT = mybir.ActivationFunctionType

P = 128
PACK = 4
PASS = P * PACK
PASSES = 2
BANK = 512
BANKS = 8
QUADRANTS = 4
STRIPE = 16
CHUNKS = S // BANK
TILES = H // P
LAST = TILES - 1
H_AHEAD = 4
HALF = KEPT // 2
W1_STEPS = (0, 2)
W4_STEP = TILES - 4
FIRST_HALF_STEP = TILES - 3


def tile_list_provenance_chain_features_kernel(
    tc, tab_words, tab_scales, offs, pos1, pos2, pos3, pos4, w1, gain, link, w4_words, w4_scales, skip,
    out_0, out_1, out_2,
):
    nc = tc.nc
    with ExitStack() as ctx:
        keep = ctx.enter_context(tc.tile_pool(name="keep", bufs=1))
        ring = ctx.enter_context(tc.tile_pool(name="ring", bufs=1))
        psum = ctx.enter_context(tc.psum_pool(name="psum", bufs=1))

        def load_list(name, source):
            tile = keep.tile(list(source.shape), U16, name=name)
            nc.sync.dma_start(tile[:], source)
            return tile

        def load_table_words(a):
            tile = ring.tile([P, T], U32, name="tab_words%d" % a, tag="wide", bufs=2, align_bytes=64)
            source = tab_words[a].rearrange("p t i -> p (t i)").bitcast(I32)
            for part in range(2):
                cols = slice(part * T // 2, (part + 1) * T // 2)
                nc.sync.dma_start(tile[:].bitcast(I32)[:, cols], source[:, cols])
            return tile

        def load_w1(a, b, pieces=1):
            tile = ring.tile([P, PACK, PASS], F32, name="w1_%d%d" % (a, b), tag="rows", bufs=4, align_bytes=64)
            source = w1[a * PASS : (a + 1) * PASS, b * PASS : (b + 1) * PASS]
            source = source.rearrange("(p j) n -> p j n", j=PACK)
            for piece in range(pieces):
                cols = slice(piece * PASS // pieces, (piece + 1) * PASS // pieces)
                nc.sync.dma_start(tile[:, :, cols], source[:, :, cols])
            return tile

        def load_per_row(name, source):
            tile = keep.tile([P, TILES], F32, name=name)
            nc.sync.dma_start(
                tile[:].rearrange("p (b t) -> p b t", t=PACK), source.rearrange("(b p t) -> p b t", p=P, t=PACK)
            )
            return tile

        def load_link(tile, b, ts):
            source = link[b * PASS : (b + 1) * PASS, :].rearrange("(p t) m -> p t m", t=PACK)
            nc.sync.dma_start(tile[:, ts, :], source[:, ts, :])

        tab_plane = keep.tile([P, T], U8, name="tab_plane", align_bytes=64)
        nc.vector.memset(tab_plane[:].bitcast(I32)[:, : T // 8], 0)
        nc.gpsimd.memset(tab_plane[:].bitcast(I32)[:, T // 8 :], 0)
        for quad in range(QUADRANTS):
            nc.sync.dma_start(
                tab_plane[32 * quad : 32 * quad + 8, :].bitcast(I32),
                tab_scales[:, 4 * quad : 4 * quad + 4, :].bitcast(I32),
            )
        w4_rows = keep.tile([P, PASS], U8, name="w4_rows", align_bytes=64)
        nc.gpsimd.memset(w4_rows[:].bitcast(I32), 0)
        w4_plane = keep.tile([P, PASSES, PASSES, PASS], U8, name="w4_plane", align_bytes=64)
        nc.gpsimd.memset(w4_plane[:].bitcast(I32), 0)

        idx = load_list("idx", offs)
        gain_sb = load_per_row("gain_sb", gain)
        tab_w = [load_table_words(0)]
        w1_raw = {(0, 0): load_w1(0, 0)}
        tab_w.append(load_table_words(1))
        w1_raw[(1, 0)] = load_w1(1, 0, pieces=2)
        p2 = load_list("p2", pos2)
        p4 = load_list("p4", pos4)
        p1 = load_list("p1", pos1)
        p3 = load_list("p3", pos3)
        skip_sb = load_per_row("skip_sb", skip)
        for quad in range(QUADRANTS):
            nc.sync.dma_start(
                w4_rows[32 * quad : 32 * quad + 16, :].bitcast(I32),
                w4_scales[:, 4 * quad : 4 * quad + 4, :].rearrange("a r (b n) -> (r b) a n", n=PASS).bitcast(I32),
            )

        banks = [psum.tile([P, BANK], F32, name="bank%d" % n) for n in range(BANKS)]

        got_w0 = keep.tile([P, S], U32, name="got_w0", align_bytes=64)
        nc.vector.tensor_copy(got_w0[:], tab_w[0][:].indirect(idx[:]))
        got_plane = keep.tile([P, S], U8, name="got_plane", align_bytes=64)
        nc.vector.tensor_copy(got_plane[:], tab_plane[:].indirect(idx[:]))

        w1_codes, w1_plane = {}, {}

        def round_w1(a, b, u, pieces=1, room=None):
            if room is None:
                room = ring.tile([P, BANK], F32, name="w1_room", tag="w1_room", bufs=3, align_bytes=64)[:]
            rounded = room.bitcast(BF16)
            for piece in range(pieces):
                qs = slice(piece * P // pieces, (piece + 1) * P // pieces)
                nc.scalar.copy(
                    rounded.rearrange("p (t q j) -> p q j t", t=2, j=PACK)[:, qs],
                    w1_raw[(a, b)][:].rearrange("p j (q t) -> p q j t", t=PACK)[:, qs, :, 2 * u : 2 * u + 2],
                )
            return rounded

        def quantize_w1(a, b, u, rounded, codes=None):
            if codes is None:
                codes = keep.tile([P, 2 * P], U32, name="w1_codes%d%d" % (a, u), align_bytes=64)[:]
            plane = keep.tile([P, 2 * P], U8, name="w1_plane%d%d%d" % (a, b, u), align_bytes=64)
            nc.vector.quantize_mx(out=codes.bitcast(FP8X4), scales=plane[:], in_=rounded)
            w1_codes[(a, b, u)] = codes
            w1_plane[(a, b, u)] = plane

        got_w1 = []

        def pick_words_of_pass_1(c, tile):
            entries = idx[:, c * (BANK // STRIPE) : (c + 1) * (BANK // STRIPE)]
            nc.vector.tensor_copy(tile[:], tab_w[1][:].indirect(entries))
            got_w1.append(tile)

        quantize_w1(0, 0, 0, round_w1(0, 0, 0))
        for c in range(CHUNKS - 1):
            pick_words_of_pass_1(c, keep.tile([P, BANK], U32, name="got_w1_%d" % c, align_bytes=64))
        first_room = keep.tile([P, BANK], F32, name="first_room", tag="handover", align_bytes=64)
        quantize_w1(1, 0, 0, round_w1(1, 0, 0, pieces=2, room=first_room[:]))
        pick_words_of_pass_1(CHUNKS - 1, keep.tile([P, BANK], U32, name="got_w1_last", tag="handover", align_bytes=64))

        link_sb = [
            ring.tile([P, PACK, PAIRS], F32, name="link%d" % b, tag="wide", bufs=2, align_bytes=64) for b in range(PASSES)
        ]
        load_link(link_sb[0], 0, slice(0, 2))
        w1_raw[(0, 1)] = load_w1(0, 1)
        w1_raw[(1, 1)] = load_w1(1, 1)
        load_link(link_sb[0], 0, slice(2, PACK))
        w4_raw = keep.tile([P, PASSES, 2 * H], U8, name="w4_raw", align_bytes=64)
        nc.sync.dma_start(w4_raw[:].bitcast(I32), w4_words.rearrange("a p n -> p a n").bitcast(I32))
        load_link(link_sb[1], 1, slice(0, PACK))

        spare = [keep.tile([P, BANK], F32, name="spare%d" % n, align_bytes=64) for n in range(CHUNKS)]
        a2 = [keep.tile([P, PACK, KEPT], F32, name="a2_%d" % b, align_bytes=64) for b in range(PASSES)]
        kept = [keep.tile([P, KEPT], F32, name="kept")] * LAST + [spare[2]]
        h = []

        def gelu_buffer(i, c):
            if i == 0:
                return spare[c][:]
            if c < CHUNKS - 1:
                return ring.tile([P, BANK], F32, name="curved", tag="curved", bufs=2)[:]
            if i == 1:
                return kept[0][:]
            if i - 2 in W1_STEPS or i - 2 == FIRST_HALF_STEP:
                return keep.tile([P, BANK], F32, name="curved", tag="step%d" % (i - 2), align_bytes=64)[:]
            return a2[(i - 2) // PACK][:, (i - 2) % PACK, :]

        def first_stage(i):
            b, t = divmod(i, PACK)
            u, cols = t // 2, slice((t % 2) * P, (t % 2 + 1) * P)
            h_i = ring.tile([P, S], F32, name="h", tag="h", bufs=H_AHEAD)
            for c in range(CHUNKS):
                bank = banks[(CHUNKS * i + c) % BANKS]
                chunk = slice(c * BANK, (c + 1) * BANK)
                for a in range(PASSES):
                    moving = got_w0[:, chunk] if a == 0 else got_w1[c][:]
                    nc.tensor.matmul_mx(
                        out=bank[:],
                        lhsT=w1_codes[(a, b, u)][:, cols].bitcast(FP8X4),
                        lhsT_scale=w1_plane[(a, b, u)][:, cols],
                        rhs=moving.bitcast(FP8X4),
                        rhs_scale=got_plane[4 * a : P, chunk],
                        start=(a == 0),
                        stop=(a == PASSES - 1),
                    )
                curved = gelu_buffer(i, c)
                nc.scalar.activation(curved, bank[:], ACT.Gelu_apprx_tanh)
                if i == 0:
                    nc.vector.tensor_scalar(h_i[:, chunk], curved, gain_sb[:, 0:1], None, ALU.mult)
                else:
                    nc.scalar.activation(h_i[:, chunk], curved, ACT.Copy, scale=gain_sb[:, i : i + 1])
            h.append(h_i)

        second = keep.tile([P, PAIRS], F32, name="second")
        diff = keep.tile([P, PAIRS], F32, name="diff", tag="diff", align_bytes=64)
        entry = [keep.tile([P, KEPT], F32, name="entry")] * LAST + [spare[0]]
        a1 = []

        def pick_second(i):
            nc.vector.tensor_copy(second[:], h[i][:].indirect(p2[:]))

        def subtract(i):
            nc.vector.tensor_tensor(diff[:], h[i][:].indirect(p1[:]), second[:], ALU.subtract)

        def times_link(i):
            a1.append(ring.tile([P, PAIRS], F32, name="a1", tag="a1", bufs=2))
            nc.gpsimd.tensor_tensor(a1[i][:], diff[:], link_sb[i // PACK][:, i % PACK, :], ALU.mult)

        def pick_entry(i):
            nc.vector.tensor_copy(entry[i][:], h[i][:].indirect(p4[:]))

        def pick_kept(i, cols=slice(0, KEPT)):
            entries = p3[:, cols.start // STRIPE : cols.stop // STRIPE]
            nc.vector.tensor_copy(kept[i][:, cols], a1[i][:].indirect(entries))

        def larger(i, cols=slice(0, KEPT)):
            nc.vector.tensor_tensor(a2[i // PACK][:, i % PACK, cols], kept[i][:, cols], entry[i][:, cols], ALU.max)

        halves = [slice(half * HALF, (half + 1) * HALF) for half in range(2)]

        def interleave(copy, planar, room=None):
            if room is None:
                room = ring.tile([P, BANK], F32, name="room", tag="room", bufs=4, align_bytes=64)[:]
            rounded = room.bitcast(BF16)
            copy(rounded.rearrange("p (c e t) -> p c t e", e=4, t=PACK), planar.rearrange("p t (c e) -> p c t e", e=4))
            return rounded

        def quantize(codes, plane, rounded):
            nc.vector.quantize_mx(out=codes.bitcast(FP8X4), scales=plane, in_=rounded)

        def sums(i, half):
            return banks[(BANKS // 2) * half + i // 2][:, halves[i % 2]]

        def quantize_and_multiply(a, half, rounded, tag):
            codes = keep.tile([P, HALF], U32, name="a2_codes", tag=tag, align_bytes=64)
            plane = keep.tile([P, HALF], U8, name="a2_plane%d%d" % (a, half), align_bytes=64)
            quantize(codes[:], plane[:], rounded)
            for i in range(TILES):
                nc.tensor.matmul_mx(
                    out=sums(i, half),
                    lhsT=w4_codes[:, a, 2 * P * i : 2 * P * (i + 1)].bitcast(FP4X4),
                    lhsT_scale=w4_plane[:, i // PACK, a, P * (i % PACK) : P * (i % PACK + 1)],
                    rhs=codes[:].bitcast(FP8X4),
                    rhs_scale=plane[:],
                    start=(a == 0 and i % 2 == 0),
                    stop=(a == PASSES - 1 and i % 2 == 1),
                )

        first_stage(0)
        quantize_w1(0, 0, 1, round_w1(0, 0, 1))
        quantize_w1(1, 0, 1, round_w1(1, 0, 1, room=spare[1][:]))
        w4_rows_dealt = keep.tile([P, PASS], U8, name="w4_rows_dealt", align_bytes=64)
        nc.vector.tensor_copy(
            w4_rows_dealt[:].rearrange("p (t q) -> p t q", t=PACK), w4_rows[:].rearrange("p (q t) -> p t q", t=PACK)
        )
        for quad in range(QUADRANTS):
            nc.sync.dma_start(
                w4_plane[32 * quad : 32 * quad + 4].rearrange("r b a n -> r (b a) n").bitcast(I32),
                w4_rows_dealt[32 * quad : 32 * quad + 16, :].bitcast(I32),
            )
        pick_second(0)
        subtract(0)
        times_link(0)
        first_stage(1)
        pick_second(1)

        for i in range(TILES - 2):
            subtract(i + 1)
            times_link(i + 1)
            pick_kept(i)
            pick_entry(i)
            if i in W1_STEPS:
                w1_rounded = [round_w1(0, 1, i // 2, room=a2[0][:, i, :]), round_w1(1, 1, i // 2)]
            if i == W4_STEP:
                w4_codes = keep.tile([P, PASSES, 2 * H], U8, name="w4_codes", align_bytes=64)
                nc.scalar.copy(
                    w4_codes[:].bitcast(U16).rearrange("p a (b t q) -> p (a b) t q", t=PACK, q=P),
                    w4_raw[:].bitcast(U16).rearrange("p a (b q t) -> p (a b) t q", t=PACK, q=P),
                )
            if i == FIRST_HALF_STEP:
                first_half = interleave(nc.scalar.copy, a2[0][:, :, halves[0]], room=a2[1][:, i % PACK, :])
            first_stage(i + 2)
            pick_second(i + 2)
            if i in W1_STEPS:
                codes = keep.tile([P, PASSES, 2 * P], U32, name="w1_codes", tag="step%d" % i, align_bytes=64)
                for a in range(PASSES):
                    quantize_w1(a, 1, i // 2, w1_rounded[a], codes[:, a, :])
            if i == FIRST_HALF_STEP:
                quantize_and_multiply(0, 0, first_half, "step%d" % i)
            larger(i)

        second_half = interleave(nc.scalar.copy, a2[0][:, :, halves[1]])
        subtract(LAST)
        times_link(LAST)
        pick_kept(LAST - 1)
        pick_entry(LAST - 1)
        pick_entry(LAST)
        larger(LAST - 1)
        quantize_and_multiply(0, 1, second_half, "diff")
        for half in range(2):
            pick_kept(LAST, halves[half])
        for half in range(2):
            larger(LAST, halves[half])
        a2_rounded = [
            interleave(nc.scalar.copy, a2[1][:, :, halves[0]]),
            interleave(nc.vector.tensor_copy, a2[1][:, :, halves[1]]),
        ]
        for half in range(2):
            quantize_and_multiply(1, half, a2_rounded[half], "a2_codes1%d" % half)

        y_plane = keep.tile([P, PASSES, KEPT], U8, name="y_plane", align_bytes=64)
        y_rounded = {}
        for half in range(2):
            for b in range(PASSES):
                y = ring.tile([P, PACK, HALF], F32, name="y", tag="rows", bufs=4, align_bytes=64)
                target = out_0[b * PASS : (b + 1) * PASS, halves[half]].rearrange("(p t) j -> p t j", t=PACK)
                for t in range(PACK):
                    i = PACK * b + t
                    nc.vector.scalar_tensor_tensor(
                        y[:, t, :], a2[b][:, t, halves[half]], skip_sb[:, i : i + 1], sums(i, half), ALU.mult, ALU.add
                    )
                    if t % 2:
                        nc.sync.dma_start(target[:, t - 1 : t + 1, :], y[:, t - 1 : t + 1, :])
                last_quarter = half == 1 and b == PASSES - 1
                y_rounded[(half, b)] = interleave(nc.vector.tensor_copy if last_quarter else nc.scalar.copy, y[:])
        for half in range(2):
            for b in range(PASSES):
                codes = keep.tile([P, HALF], U32, name="y_codes%d%d" % (half, b), align_bytes=64)
                quantize(codes[:], y_plane[:, b, halves[half]], y_rounded[(half, b)])
                y_words = out_1[b].rearrange("p m t -> p (m t)").bitcast(I32)
                nc.sync.dma_start(y_words[:, halves[half]], codes[:].bitcast(I32))
        for quad in range(QUADRANTS):
            queue = nc.scalar if quad % 2 else nc.sync
            queue.dma_start(
                out_2[:, 4 * quad : 4 * quad + 4, :].rearrange("g r m -> r g m").bitcast(I32),
                y_plane[32 * quad : 32 * quad + 4, :, :].bitcast(I32),
            )
